import numpy as np
import ml_dtypes


def mxq(x, axis, fmt="e4m3"):
    dtype, down = {"e4m3": (ml_dtypes.float8_e4m3fn, 7), "e5m2": (ml_dtypes.float8_e5m2, 14)}[fmt]
    v = np.moveaxis(np.asarray(x, np.float32).astype(ml_dtypes.bfloat16).astype(np.float64), axis, -1)
    blocks = v.reshape(v.shape[:-1] + (-1, 32))
    amax = np.abs(blocks).max(-1, keepdims=True)
    byte = np.maximum(np.where(amax > 0, np.frexp(amax)[1] - 1 + 127, 0) - down, 1)
    scale = np.exp2(byte - 127.0)
    codes = (blocks / scale).astype(np.float32).astype(dtype).astype(np.float64)
    return np.moveaxis((codes * scale).reshape(v.shape), -1, axis)


WIDE = False


def mx_kscale(k):
    if not WIDE:
        return np.ones(k)
    levels = np.array([10, -10, 5, -5, 0])
    if k % 512:
        return np.exp2(np.random.permutation(np.resize(levels, k // 32))).repeat(32)
    a = np.empty((k // 512, 16))
    for p in range(k // 512):
        a[p, :8] = np.random.permutation(np.resize(levels, 8))
        for g in range(8):
            far = levels[np.abs(levels - a[p, g]) >= 10]
            a[p, g + 8] = far[np.random.randint(len(far))]
    return np.exp2(a.ravel()).repeat(32)


def f64(x):
    return np.asarray(x).astype(np.float64)


def striped8(idx):
    return np.asarray(idx).reshape(8, -1, 16).transpose(0, 2, 1).reshape(128, -1).astype(np.uint16)


def unstriped8(offs):
    return offs.reshape(8, 16, -1).transpose(0, 2, 1).reshape(8, -1).astype(np.int64)


def pick8(x, idx, run):
    r = np.arange(len(x))
    return x[r[:, None], idx[r % (8 * run) // run]]


E2M1 = np.array([0.0, 0.5, 1.0, 1.5, 2.0, 3.0, 4.0, 6.0, -0.0, -0.5, -1.0, -1.5, -2.0, -3.0, -4.0, -6.0])


def pack_weight(w, fmt):
    k, n = w.shape
    w = f64(np.asarray(w, np.float32).astype(ml_dtypes.bfloat16)).reshape(k // 32, 32, n)
    amax = np.abs(w).max(1)
    if fmt == "e4m3":
        byte = np.frexp(amax)[1] - 1 + 127 - 7
    else:
        mant, ex = np.frexp(amax / 6.0)
        byte = np.where(mant > 0.5, ex, ex - 1) + 127
    byte = np.clip(np.where(amax > 0, byte, 1), 1, 254)
    scaled = (w * np.exp2(127.0 - byte)[:, None, :]).reshape(k, n).astype(np.float32)
    by_word = np.ascontiguousarray(scaled.reshape(k // 512, 128, 4, n).transpose(0, 1, 3, 2))
    if fmt == "e4m3":
        words = by_word.astype(ml_dtypes.float8_e4m3fn).view(np.uint8)
    else:
        c = by_word.astype(ml_dtypes.float4_e2m1fn).view(np.uint8) & 0xF
        words = (c[..., 0::2] | (c[..., 1::2] << 4)).reshape(k // 512, 128, 2 * n)
    return np.ascontiguousarray(words), np.ascontiguousarray(byte.astype(np.uint8).reshape(k // 512, 16, n))


def unpack_weight(words, scales, fmt):
    g, _, n = scales.shape
    words = np.ascontiguousarray(words).reshape(g, 128, n, -1)
    if fmt == "e4m3":
        vals = words.view(ml_dtypes.float8_e4m3fn).astype(np.float64)
    else:
        nib = np.empty((g, 128, n, 4), np.uint8)
        nib[..., 0::2] = words & 0xF
        nib[..., 1::2] = words >> 4
        vals = E2M1[nib]
    vals = vals * np.repeat(np.exp2(scales.astype(np.float64) - 127.0), 8, axis=1)[..., None]
    return vals.transpose(0, 1, 3, 2).reshape(g * 512, n)


D, K, T, I, Q = 512, 512, 1024, 512, 128


def setup_inputs():
    n = np.random.standard_normal
    idx = np.stack([np.random.permutation(T)[:I] for _ in range(8)])
    idx2 = np.stack([np.random.permutation(T)[:I] for _ in range(8)])
    idx3 = np.stack([np.random.permutation(T)[:I] for _ in range(8)])
    idx4 = np.stack([np.random.permutation(T)[:I] for _ in range(8)])
    fd = mx_kscale(D)
    fk = mx_kscale(K)
    wqp = pack_weight(n((D, K)) * 1.0 / np.sqrt(D) * fd[:, None] * fk, "e4m3")
    keysp = pack_weight(n((K, T)) * 1.0 / np.sqrt(K) / fk[:, None], "e2m1")
    tagsp = pack_weight(n((D, T)) * 0.5 / np.sqrt(D) * fd[:, None], "e4m3")
    return {
        "states": (n((D, Q)) * 0.95 / fd[:, None]).astype(np.float32),
        "wq_words": wqp[0],
        "wq_scales": wqp[1],
        "keys_words": keysp[0],
        "keys_scales": keysp[1],
        "tags_words": tagsp[0],
        "tags_scales": tagsp[1],
        "offs": striped8(idx),
        "offs2": striped8(idx2),
        "offs3": striped8(idx3),
        "offs4": striped8(idx4),
    }


def reference(states, wq_words, wq_scales, keys_words, keys_scales, tags_words, tags_scales, offs, offs2, offs3, offs4):
    idx = unstriped8(offs)
    idx2 = unstriped8(offs2)
    idx3 = unstriped8(offs3)
    idx4 = unstriped8(offs4)
    wqu = unpack_weight(wq_words, wq_scales, "e4m3")
    keysu = unpack_weight(keys_words, keys_scales, "e2m1")
    tagsu = unpack_weight(tags_words, tags_scales, "e4m3")
    statesq = mxq(f64(states), 0, "e4m3")
    qv = wqu.T @ statesq
    qvq = mxq(qv, 0, "e4m3")
    a = qvq.T @ keysu + statesq.T @ tagsu
    ta = np.max(a, axis=1, keepdims=True)
    e1 = np.exp(pick8(a, idx, 16) - ta)
    f1 = np.zeros((Q, T))
    f1[np.arange(Q)[:, None], idx2[np.arange(Q) % 128 // 16]] = e1
    f2 = np.zeros((Q, T))
    f2[np.arange(Q)[:, None], idx3[np.arange(Q) % 128 // 16]] = e1
    r = f1 - f2
    cc = a + r * 4.0
    y = pick8(cc, idx4, 16)
    return y

@@ -1,0 +1,164 @@
+from contextlib import ExitStack
+
+import concourse.mybir as mybir
+
+D, K, T, SLOTS, Q = 512, 512, 1024, 512, 128
+FLOPS = 2 * D * K * Q + 2 * K * Q * T + 2 * D * Q * T
+
+F32 = mybir.dt.float32
+BF16 = mybir.dt.bfloat16
+I32 = mybir.dt.int32
+U32 = mybir.dt.uint32
+U16 = mybir.dt.uint16
+U8 = mybir.dt.uint8
+FP8X4 = mybir.dt.float8_e4m3fn_x4
+FP4X4 = mybir.dt.float4_e2m1fn_x4
+ALU = mybir.AluOpType
+ACT = mybir.ActivationFunctionType
+AXIS = mybir.AxisListType
+
+P = 128
+PACK = 4
+BANK = 512
+HALF = SLOTS // 2
+LIST_COLS = SLOTS // 16
+
+
+def load_scale_rows(nc, plane, scales):
+    for quad in range(4):
+        nc.sync.dma_start(
+            out=plane[32 * quad : 32 * quad + 4, :].bitcast(I32),
+            in_=scales[0, 4 * quad : 4 * quad + 4, :].bitcast(I32),
+        )
+
+
+def tile_attend_giveandtake_madeparts_kernel(
+    tc, states, wq_words, wq_scales, keys_words, keys_scales, tags_words, tags_scales, offs, offs2, offs3, offs4, out
+):
+    nc = tc.nc
+    with ExitStack() as ctx:
+        sb = ctx.enter_context(tc.tile_pool(name="sb", bufs=1))
+        ps = ctx.enter_context(tc.psum_pool(name="ps", bufs=1))
+
+        wq_plane_raw = sb.tile([P, K], U8, align_bytes=64)
+        tags_plane = sb.tile([P, T], U8, align_bytes=64)
+        keys_plane = sb.tile([P, T], U8, align_bytes=64)
+        given = sb.tile([P, T], F32)
+        taken = sb.tile([P, T], F32)
+        fours = sb.tile([P, HALF], F32)
+        for plane in (wq_plane_raw, tags_plane, keys_plane):
+            nc.vector.memset(plane[:].bitcast(I32), 0)
+
+        states_raw = sb.tile([P, PACK, Q], F32)
+        wq_raw = sb.tile([P, K], U32)
+        keys_codes = sb.tile([P, 2 * T], U8, align_bytes=64)
+        tags_codes = sb.tile([P, T], U32, align_bytes=64)
+        nc.sync.dma_start(out=states_raw[:], in_=states.rearrange("(p j) q -> p j q", j=PACK))
+        load_scale_rows(nc, wq_plane_raw, wq_scales)
+        nc.sync.dma_start(out=wq_raw[:].bitcast(I32), in_=wq_words[0].rearrange("p n t -> p (n t)").bitcast(I32))
+        nc.sync.dma_start(out=tags_codes[:].bitcast(I32), in_=tags_words[0].rearrange("p n t -> p (n t)").bitcast(I32))
+        nc.sync.dma_start(out=keys_codes[:].bitcast(I32), in_=keys_words[0].bitcast(I32))
+        load_scale_rows(nc, tags_plane, tags_scales)
+        load_scale_rows(nc, keys_plane, keys_scales)
+        fetch_list = sb.tile([P, LIST_COLS], U16)
+        give_list = sb.tile([P, LIST_COLS], U16)
+        take_list = sb.tile([P, LIST_COLS], U16)
+        out_list = sb.tile([P, LIST_COLS], U16)
+        for tile, src in ((fetch_list, offs), (give_list, offs2), (take_list, offs3), (out_list, offs4)):
+            nc.sync.dma_start(tile[:], src)
+
+        nc.vector.memset(given[:], 0.0)
+        nc.vector.memset(taken[:], 0.0)
+        nc.vector.memset(fours[:], 4.0)
+
+        wq_plane = sb.tile([P, K], U8, align_bytes=64)
+        wq_codes = sb.tile([P, K], U32, align_bytes=64)
+        nc.vector.tensor_copy(
+            out=wq_plane[:].rearrange("p (j m) -> p m j", j=PACK), in_=wq_plane_raw[:].rearrange("p (m j) -> p m j", j=PACK)
+        )
+        nc.scalar.copy(
+            out=wq_codes[:].rearrange("p (j m) -> p m j", j=PACK), in_=wq_raw[:].rearrange("p (m j) -> p m j", j=PACK)
+        )
+
+        states_bf = sb.tile([P, Q, PACK], BF16, align_bytes=64)
+        states_codes = sb.tile([P, Q], U32, align_bytes=64)
+        states_plane = sb.tile([P, Q], U8, align_bytes=64)
+        nc.vector.tensor_copy(out=states_bf[:], in_=states_raw[:].rearrange("p j q -> p q j"))
+        nc.vector.quantize_mx(
+            out=states_codes[:].bitcast(FP8X4), scales=states_plane[:], in_=states_bf[:].rearrange("p q j -> p (q j)")
+        )
+
+        qv_ps = ps.tile([P, PACK, Q], F32)
+        for j in range(PACK):
+            cols = slice(j * P, (j + 1) * P)
+            nc.tensor.matmul_mx(
+                out=qv_ps[:, j, :],
+                lhsT=wq_codes[:, cols].bitcast(FP8X4),
+                lhsT_scale=wq_plane[:, cols],
+                rhs=states_codes[:].bitcast(FP8X4),
+                rhs_scale=states_plane[:],
+                start=True,
+                stop=True,
+            )
+        score_ps = [ps.tile([P, BANK], F32, name=f"score_ps{b}") for b in range(T // BANK)]
+        for b in range(T // BANK):
+            cols = slice(b * BANK, (b + 1) * BANK)
+            nc.tensor.matmul_mx(
+                out=score_ps[b][:],
+                lhsT=states_codes[:].bitcast(FP8X4),
+                lhsT_scale=states_plane[:],
+                rhs=tags_codes[:, cols].bitcast(FP8X4),
+                rhs_scale=tags_plane[:, cols],
+                start=True,
+                stop=False,
+            )
+
+        qv_bf = sb.tile([P, Q, PACK], BF16, align_bytes=64)
+        qv_codes = sb.tile([P, Q], U32, align_bytes=64)
+        qv_plane = sb.tile([P, Q], U8, align_bytes=64)
+        nc.scalar.copy(out=qv_bf[:], in_=qv_ps[:].rearrange("p j q -> p q j"))
+        nc.vector.quantize_mx(
+            out=qv_codes[:].bitcast(FP8X4), scales=qv_plane[:], in_=qv_bf[:].rearrange("p q j -> p (q j)")
+        )
+
+        scores = sb.tile([P, T], F32)
+        bank_max = sb.tile([P, T // BANK], F32)
+        neg_max = sb.tile([P, 1], F32)
+        for b in range(T // BANK):
+            cols = slice(b * BANK, (b + 1) * BANK)
+            nc.tensor.matmul_mx(
+                out=score_ps[b][:],
+                lhsT=qv_codes[:].bitcast(FP8X4),
+                lhsT_scale=qv_plane[:],
+                rhs=keys_codes[:, 2 * b * BANK : 2 * (b + 1) * BANK].bitcast(FP4X4),
+                rhs_scale=keys_plane[:, cols],
+                start=False,
+                stop=True,
+            )
+            nc.vector.tensor_scalar(
+                out=scores[:, cols], in0=score_ps[b][:], scalar1=1.0, scalar2=None, op0=ALU.mult, op1=ALU.max,
+                accum_out=bank_max[:, b : b + 1],
+            )
+        nc.vector.tensor_reduce(out=neg_max[:], in_=bank_max[:], axis=AXIS.X, op=ALU.max, negate=True)
+
+        halves = [(slice(h * HALF, (h + 1) * HALF), slice(h * HALF // 16, (h + 1) * HALF // 16)) for h in range(2)]
+        e1 = sb.tile([P, SLOTS], F32)
+        for slots, entries in halves:
+            nc.scalar.activation(
+                out=e1[:, slots], in_=scores[:].indirect(fetch_list[:, entries]), func=ACT.Exp, bias=neg_max[:]
+            )
+        for slots, entries in halves:
+            nc.vector.tensor_tensor(given[:].indirect(give_list[:, entries]), e1[:, slots], fours[:], ALU.mult)
+        nc.vector.tensor_copy(taken[:].indirect(take_list[:]), e1[:])
+        with_given = sb.tile([P, T], F32)
+        cc = sb.tile([P, T], F32)
+        nc.gpsimd.tensor_tensor(with_given[:], scores[:], given[:], ALU.add)
+        nc.vector.scalar_tensor_tensor(
+            out=cc[:], in0=taken[:], scalar=-4.0, in1=with_given[:], op0=ALU.mult, op1=ALU.add
+        )
+
+        picked = [sb.tile([P, HALF], F32, name=f"picked{h}") for h in range(2)]
+        nc.vector.tensor_copy(picked[0][:], cc[:].indirect(out_list[:, halves[0][1]]))
+        nc.scalar.activation(picked[1][:], cc[:].indirect(out_list[:, halves[1][1]]), ACT.Copy)
+        nc.sync.dma_start(out=out[:, halves[0][0]], in_=picked[0][:])
+        nc.scalar.dma_start(out=out[:, halves[1][0]], in_=picked[1][:])

@@ -24,12 +24,12 @@ HALF = SLOTS // 2
 LIST_COLS = SLOTS // 16
 
 
-def load_scale_rows(nc, plane, scales):
-    for quad in range(4):
-        nc.sync.dma_start(
-            out=plane[32 * quad : 32 * quad + 4, :].bitcast(I32),
-            in_=scales[0, 4 * quad : 4 * quad + 4, :].bitcast(I32),
-        )
+def load_scale_rows(queue, plane, scales, quad):
+    rows = scales[0, 4 * quad : 4 * quad + 4, :].bitcast(I32)
+    queue.dma_start(
+        out=plane[32 * quad : 32 * quad + 32, :].bitcast(I32),
+        in_=rows.unsqueeze(0).broadcast_to([8, 4, scales.shape[2] // 4]),
+    )
 
 
 def tile_attend_giveandtake_madeparts_kernel(
@@ -46,20 +46,21 @@ def tile_attend_giveandtake_madeparts_kernel(
         given = sb.tile([P, T], F32)
         taken = sb.tile([P, T], F32)
         fours = sb.tile([P, HALF], F32)
-        for plane in (wq_plane_raw, tags_plane, keys_plane):
-            nc.vector.memset(plane[:].bitcast(I32), 0)
 
         states_raw = sb.tile([P, PACK, Q], F32)
         wq_raw = sb.tile([P, K], U32)
         keys_codes = sb.tile([P, 2 * T], U8, align_bytes=64)
         tags_codes = sb.tile([P, T], U32, align_bytes=64)
-        nc.sync.dma_start(out=states_raw[:], in_=states.rearrange("(p j) q -> p j q", j=PACK))
-        load_scale_rows(nc, wq_plane_raw, wq_scales)
         nc.sync.dma_start(out=wq_raw[:].bitcast(I32), in_=wq_words[0].rearrange("p n t -> p (n t)").bitcast(I32))
+        for quad in range(4):
+            load_scale_rows(nc.sync, wq_plane_raw, wq_scales, quad)
+        nc.sync.dma_start(out=states_raw[:], in_=states.rearrange("(p j) q -> p j q", j=PACK))
         nc.sync.dma_start(out=tags_codes[:].bitcast(I32), in_=tags_words[0].rearrange("p n t -> p (n t)").bitcast(I32))
+        for quad in range(4):
+            load_scale_rows(nc.sync, tags_plane, tags_scales, quad)
         nc.sync.dma_start(out=keys_codes[:].bitcast(I32), in_=keys_words[0].bitcast(I32))
-        load_scale_rows(nc, tags_plane, tags_scales)
-        load_scale_rows(nc, keys_plane, keys_scales)
+        for quad in range(4):
+            load_scale_rows(nc.sync if quad < 2 else nc.gpsimd, keys_plane, keys_scales, quad)
         fetch_list = sb.tile([P, LIST_COLS], U16)
         give_list = sb.tile([P, LIST_COLS], U16)
         take_list = sb.tile([P, LIST_COLS], U16)
@@ -83,10 +84,15 @@ def tile_attend_giveandtake_madeparts_kernel(
         states_bf = sb.tile([P, Q, PACK], BF16, align_bytes=64)
         states_codes = sb.tile([P, Q], U32, align_bytes=64)
         states_plane = sb.tile([P, Q], U8, align_bytes=64)
-        nc.vector.tensor_copy(out=states_bf[:], in_=states_raw[:].rearrange("p j q -> p q j"))
-        nc.vector.quantize_mx(
-            out=states_codes[:].bitcast(FP8X4), scales=states_plane[:], in_=states_bf[:].rearrange("p q j -> p (q j)")
-        )
+        row_halves = [slice(h * Q // 2, (h + 1) * Q // 2) for h in range(2)]
+        for rows in row_halves:
+            nc.vector.tensor_copy(out=states_bf[:, rows, :], in_=states_raw[:, :, rows].rearrange("p j q -> p q j"))
+        for rows in row_halves:
+            nc.vector.quantize_mx(
+                out=states_codes[:, rows].bitcast(FP8X4),
+                scales=states_plane[:, rows],
+                in_=states_bf[:, rows, :].rearrange("p q j -> p (q j)"),
+            )
 
         qv_ps = ps.tile([P, PACK, Q], F32)
         for j in range(PACK):
@@ -116,10 +122,13 @@ def tile_attend_giveandtake_madeparts_kernel(
         qv_bf = sb.tile([P, Q, PACK], BF16, align_bytes=64)
         qv_codes = sb.tile([P, Q], U32, align_bytes=64)
         qv_plane = sb.tile([P, Q], U8, align_bytes=64)
-        nc.scalar.copy(out=qv_bf[:], in_=qv_ps[:].rearrange("p j q -> p q j"))
-        nc.vector.quantize_mx(
-            out=qv_codes[:].bitcast(FP8X4), scales=qv_plane[:], in_=qv_bf[:].rearrange("p q j -> p (q j)")
-        )
+        for rows in row_halves:
+            nc.scalar.copy(out=qv_bf[:, rows, :], in_=qv_ps[:, :, rows].rearrange("p j q -> p q j"))
+            nc.vector.quantize_mx(
+                out=qv_codes[:, rows].bitcast(FP8X4),
+                scales=qv_plane[:, rows],
+                in_=qv_bf[:, rows, :].rearrange("p q j -> p (q j)"),
+            )
 
         scores = sb.tile([P, T], F32)
         bank_max = sb.tile([P, T // BANK], F32)
@@ -149,13 +158,13 @@ def tile_attend_giveandtake_madeparts_kernel(
             )
         for slots, entries in halves:
             nc.vector.tensor_tensor(given[:].indirect(give_list[:, entries]), e1[:, slots], fours[:], ALU.mult)
-        nc.vector.tensor_copy(taken[:].indirect(take_list[:]), e1[:])
+        minus_four_e1 = sb.tile([P, SLOTS], F32)
+        nc.scalar.activation(minus_four_e1[:], e1[:], ACT.Copy, scale=-4.0)
+        nc.vector.tensor_copy(taken[:].indirect(take_list[:]), minus_four_e1[:])
         with_given = sb.tile([P, T], F32)
         cc = sb.tile([P, T], F32)
         nc.gpsimd.tensor_tensor(with_given[:], scores[:], given[:], ALU.add)
-        nc.vector.scalar_tensor_tensor(
-            out=cc[:], in0=taken[:], scalar=-4.0, in1=with_given[:], op0=ALU.mult, op1=ALU.add
-        )
+        nc.vector.tensor_tensor(cc[:], with_given[:], taken[:], ALU.add)
 
         picked = [sb.tile([P, HALF], F32, name=f"picked{h}") for h in range(2)]
         nc.vector.tensor_copy(picked[0][:], cc[:].indirect(out_list[:, halves[0][1]]))

@@ -21,15 +21,17 @@ P = 128
 PACK = 4
 BANK = 512
 HALF = SLOTS // 2
+PIECE = 256
+TURNED = 768
 LIST_COLS = SLOTS // 16
 
 
-def load_scale_rows(queue, plane, scales, quad):
-    rows = scales[0, 4 * quad : 4 * quad + 4, :].bitcast(I32)
-    queue.dma_start(
-        out=plane[32 * quad : 32 * quad + 32, :].bitcast(I32),
-        in_=rows.unsqueeze(0).broadcast_to([8, 4, scales.shape[2] // 4]),
-    )
+def load_scale_rows(nc, plane, scales):
+    for quad in range(4):
+        nc.sync.dma_start(
+            out=plane[32 * quad : 32 * quad + 4, :].bitcast(I32),
+            in_=scales[0, 4 * quad : 4 * quad + 4, :].bitcast(I32),
+        )
 
 
 def tile_attend_giveandtake_madeparts_kernel(
@@ -43,24 +45,26 @@ def tile_attend_giveandtake_madeparts_kernel(
         wq_plane_raw = sb.tile([P, K], U8, align_bytes=64)
         tags_plane = sb.tile([P, T], U8, align_bytes=64)
         keys_plane = sb.tile([P, T], U8, align_bytes=64)
-        given = sb.tile([P, T], F32)
-        taken = sb.tile([P, T], F32)
         fours = sb.tile([P, HALF], F32)
+        nc.vector.memset(wq_plane_raw[:].bitcast(I32), 0)
+        nc.vector.memset(tags_plane[:].bitcast(I32), 0)
+        nc.vector.memset(keys_plane[:].bitcast(I32), 0)
 
+        identity = sb.tile([P, P], F32)
+        col_less_row = sb.tile([P, P], I32)
+        nc.gpsimd.iota(col_less_row[:], pattern=[[1, P]], base=0, channel_multiplier=-1)
+        nc.vector.tensor_scalar(out=identity[:], in0=col_less_row[:], scalar1=0.0, scalar2=None, op0=ALU.is_equal)
         states_raw = sb.tile([P, PACK, Q], F32)
         wq_raw = sb.tile([P, K], U32)
         keys_codes = sb.tile([P, 2 * T], U8, align_bytes=64)
         tags_codes = sb.tile([P, T], U32, align_bytes=64)
-        nc.sync.dma_start(out=wq_raw[:].bitcast(I32), in_=wq_words[0].rearrange("p n t -> p (n t)").bitcast(I32))
-        for quad in range(4):
-            load_scale_rows(nc.sync, wq_plane_raw, wq_scales, quad)
         nc.sync.dma_start(out=states_raw[:], in_=states.rearrange("(p j) q -> p j q", j=PACK))
+        nc.sync.dma_start(out=wq_raw[:].bitcast(I32), in_=wq_words[0].rearrange("p n t -> p (n t)").bitcast(I32))
+        load_scale_rows(nc, wq_plane_raw, wq_scales)
         nc.sync.dma_start(out=tags_codes[:].bitcast(I32), in_=tags_words[0].rearrange("p n t -> p (n t)").bitcast(I32))
-        for quad in range(4):
-            load_scale_rows(nc.sync, tags_plane, tags_scales, quad)
+        load_scale_rows(nc, tags_plane, tags_scales)
         nc.sync.dma_start(out=keys_codes[:].bitcast(I32), in_=keys_words[0].bitcast(I32))
-        for quad in range(4):
-            load_scale_rows(nc.sync if quad < 2 else nc.gpsimd, keys_plane, keys_scales, quad)
+        load_scale_rows(nc, keys_plane, keys_scales)
         fetch_list = sb.tile([P, LIST_COLS], U16)
         give_list = sb.tile([P, LIST_COLS], U16)
         take_list = sb.tile([P, LIST_COLS], U16)
@@ -68,31 +72,31 @@ def tile_attend_giveandtake_madeparts_kernel(
         for tile, src in ((fetch_list, offs), (give_list, offs2), (take_list, offs3), (out_list, offs4)):
             nc.sync.dma_start(tile[:], src)
 
-        nc.vector.memset(given[:], 0.0)
-        nc.vector.memset(taken[:], 0.0)
         nc.vector.memset(fours[:], 4.0)
 
         wq_plane = sb.tile([P, K], U8, align_bytes=64)
         wq_codes = sb.tile([P, K], U32, align_bytes=64)
         nc.vector.tensor_copy(
-            out=wq_plane[:].rearrange("p (j m) -> p m j", j=PACK), in_=wq_plane_raw[:].rearrange("p (m j) -> p m j", j=PACK)
+            out=wq_plane[:].rearrange("p (j m) -> p j m", j=PACK), in_=wq_plane_raw[:].rearrange("p (m j) -> p j m", j=PACK)
         )
         nc.scalar.copy(
             out=wq_codes[:].rearrange("p (j m) -> p m j", j=PACK), in_=wq_raw[:].rearrange("p (m j) -> p m j", j=PACK)
         )
 
-        states_bf = sb.tile([P, Q, PACK], BF16, align_bytes=64)
+        states_bf = [sb.tile([P, Q // 2, PACK], BF16, name=f"states_bf{h}", tag=f"states_bf{h}", align_bytes=64) for h in range(2)]
         states_codes = sb.tile([P, Q], U32, align_bytes=64)
         states_plane = sb.tile([P, Q], U8, align_bytes=64)
         row_halves = [slice(h * Q // 2, (h + 1) * Q // 2) for h in range(2)]
-        for rows in row_halves:
-            nc.vector.tensor_copy(out=states_bf[:, rows, :], in_=states_raw[:, :, rows].rearrange("p j q -> p q j"))
-        for rows in row_halves:
+        for half_bf, rows in zip(states_bf, row_halves):
+            nc.vector.tensor_copy(out=half_bf[:], in_=states_raw[:, :, rows].rearrange("p j q -> p q j"))
+        for half_bf, rows in zip(states_bf, row_halves):
             nc.vector.quantize_mx(
                 out=states_codes[:, rows].bitcast(FP8X4),
                 scales=states_plane[:, rows],
-                in_=states_bf[:, rows, :].rearrange("p q j -> p (q j)"),
+                in_=half_bf[:].rearrange("p q j -> p (q j)"),
             )
+        given = sb.tile([P, T], F32, tag="states_bf1", align_bytes=64)
+        nc.vector.memset(given[:], 0.0)
 
         qv_ps = ps.tile([P, PACK, Q], F32)
         for j in range(PACK):
@@ -106,7 +110,7 @@ def tile_attend_giveandtake_madeparts_kernel(
                 start=True,
                 stop=True,
             )
-        score_ps = [ps.tile([P, BANK], F32, name=f"score_ps{b}") for b in range(T // BANK)]
+        score_ps = [ps.tile([P, BANK], F32, name=f"score_ps{b}", tag=f"score_ps{b}") for b in range(T // BANK)]
         for b in range(T // BANK):
             cols = slice(b * BANK, (b + 1) * BANK)
             nc.tensor.matmul_mx(
@@ -131,7 +135,7 @@ def tile_attend_giveandtake_madeparts_kernel(
             )
 
         scores = sb.tile([P, T], F32)
-        bank_max = sb.tile([P, T // BANK], F32)
+        bank_max = sb.tile([P, T // BANK], F32, tag="bank_max")
         neg_max = sb.tile([P, 1], F32)
         for b in range(T // BANK):
             cols = slice(b * BANK, (b + 1) * BANK)
@@ -149,6 +153,22 @@ def tile_attend_giveandtake_madeparts_kernel(
                 accum_out=bank_max[:, b : b + 1],
             )
         nc.vector.tensor_reduce(out=neg_max[:], in_=bank_max[:], axis=AXIS.X, op=ALU.max, negate=True)
+        taken = sb.tile([P, T], F32, tag="bank_max")
+        nc.vector.memset(taken[:], 0.0)
+
+        pieces = [slice(c * PIECE, (c + 1) * PIECE) for c in range(TURNED // PIECE)]
+        turned_ps = [ps.tile([P, PIECE], F32, name=f"turned_ps{c}") for c in range(TURNED // PIECE)]
+
+        def turn_into(bank, src, first):
+            for c in range(PIECE // P):
+                cols = slice(c * P, (c + 1) * P)
+                nc.tensor.matmul(
+                    bank[:, cols], lhsT=src[:, cols], rhs=identity[:], is_transpose=True,
+                    start=(first and c == 0), stop=(not first and c == PIECE // P - 1),
+                )
+
+        for bank, cols in zip(turned_ps, pieces):
+            turn_into(bank, scores[:, cols], True)
 
         halves = [(slice(h * HALF, (h + 1) * HALF), slice(h * HALF // 16, (h + 1) * HALF // 16)) for h in range(2)]
         e1 = sb.tile([P, SLOTS], F32)
@@ -161,10 +181,22 @@ def tile_attend_giveandtake_madeparts_kernel(
         minus_four_e1 = sb.tile([P, SLOTS], F32)
         nc.scalar.activation(minus_four_e1[:], e1[:], ACT.Copy, scale=-4.0)
         nc.vector.tensor_copy(taken[:].indirect(take_list[:]), minus_four_e1[:])
-        with_given = sb.tile([P, T], F32)
         cc = sb.tile([P, T], F32)
-        nc.gpsimd.tensor_tensor(with_given[:], scores[:], given[:], ALU.add)
-        nc.vector.tensor_tensor(cc[:], with_given[:], taken[:], ALU.add)
+        turned = sb.tile([P, TURNED], F32)
+        for bank, cols in zip(turned_ps, pieces):
+            turn_into(bank, given[:, cols], False)
+            nc.scalar.copy(out=turned[:, cols], in_=bank[:])
+        rest = slice(TURNED, T)
+        with_given = sb.tile([P, T - TURNED], F32)
+        nc.vector.tensor_tensor(with_given[:], scores[:, rest], given[:, rest], ALU.add)
+        nc.gpsimd.tensor_tensor(cc[:, rest], with_given[:], taken[:, rest], ALU.add)
+        for b, first in enumerate(range(0, TURNED, BANK)):
+            width = min(BANK, TURNED - first)
+            with_given_ps = ps.tile([P, width], F32, name=f"with_given_ps{b}", tag=f"score_ps{b}")
+            for c in range(0, width, P):
+                nc.tensor.transpose(with_given_ps[:, c : c + P], turned[:, first + c : first + c + P], identity[:])
+            cols = slice(first, first + width)
+            nc.vector.tensor_tensor(cc[:, cols], with_given_ps[:], taken[:, cols], ALU.add)
 
         picked = [sb.tile([P, HALF], F32, name=f"picked{h}") for h in range(2)]
         nc.vector.tensor_copy(picked[0][:], cc[:].indirect(out_list[:, halves[0][1]]))

from contextlib import ExitStack

import concourse.mybir as mybir

D, K, T, SLOTS, Q = 512, 512, 1024, 512, 128
FLOPS = 2 * D * K * Q + 2 * K * Q * T + 2 * D * Q * T

F32 = mybir.dt.float32
BF16 = mybir.dt.bfloat16
I32 = mybir.dt.int32
U32 = mybir.dt.uint32
U16 = mybir.dt.uint16
U8 = mybir.dt.uint8
FP8X4 = mybir.dt.float8_e4m3fn_x4
FP4X4 = mybir.dt.float4_e2m1fn_x4
ALU = mybir.AluOpType
ACT = mybir.ActivationFunctionType
AXIS = mybir.AxisListType

P = 128
PACK = 4
BANK = 512
HALF = SLOTS // 2
PIECE = 256
TURNED = 768
LIST_COLS = SLOTS // 16


def load_scale_rows(nc, plane, scales):
    for quad in range(4):
        nc.sync.dma_start(
            out=plane[32 * quad : 32 * quad + 4, :].bitcast(I32),
            in_=scales[0, 4 * quad : 4 * quad + 4, :].bitcast(I32),
        )


def tile_attend_giveandtake_madeparts_kernel(
    tc, states, wq_words, wq_scales, keys_words, keys_scales, tags_words, tags_scales, offs, offs2, offs3, offs4, out
):
    nc = tc.nc
    with ExitStack() as ctx:
        sb = ctx.enter_context(tc.tile_pool(name="sb", bufs=1))
        ps = ctx.enter_context(tc.psum_pool(name="ps", bufs=1))

        wq_plane_raw = sb.tile([P, K], U8, align_bytes=64)
        tags_plane = sb.tile([P, T], U8, align_bytes=64)
        keys_plane = sb.tile([P, T], U8, align_bytes=64)
        fours = sb.tile([P, HALF], F32)
        nc.vector.memset(wq_plane_raw[:].bitcast(I32), 0)
        nc.vector.memset(tags_plane[:].bitcast(I32), 0)
        nc.vector.memset(keys_plane[:].bitcast(I32), 0)

        identity = sb.tile([P, P], F32)
        col_less_row = sb.tile([P, P], I32)
        nc.gpsimd.iota(col_less_row[:], pattern=[[1, P]], base=0, channel_multiplier=-1)
        nc.vector.tensor_scalar(out=identity[:], in0=col_less_row[:], scalar1=0.0, scalar2=None, op0=ALU.is_equal)
        states_raw = sb.tile([P, PACK, Q], F32)
        wq_raw = sb.tile([P, K], U32)
        keys_codes = sb.tile([P, 2 * T], U8, align_bytes=64)
        tags_codes = sb.tile([P, T], U32, align_bytes=64)
        nc.sync.dma_start(out=states_raw[:], in_=states.rearrange("(p j) q -> p j q", j=PACK))
        nc.sync.dma_start(out=wq_raw[:].bitcast(I32), in_=wq_words[0].rearrange("p n t -> p (n t)").bitcast(I32))
        load_scale_rows(nc, wq_plane_raw, wq_scales)
        nc.sync.dma_start(out=tags_codes[:].bitcast(I32), in_=tags_words[0].rearrange("p n t -> p (n t)").bitcast(I32))
        load_scale_rows(nc, tags_plane, tags_scales)
        nc.sync.dma_start(out=keys_codes[:].bitcast(I32), in_=keys_words[0].bitcast(I32))
        load_scale_rows(nc, keys_plane, keys_scales)
        fetch_list = sb.tile([P, LIST_COLS], U16)
        give_list = sb.tile([P, LIST_COLS], U16)
        take_list = sb.tile([P, LIST_COLS], U16)
        out_list = sb.tile([P, LIST_COLS], U16)
        for tile, src in ((fetch_list, offs), (give_list, offs2), (take_list, offs3), (out_list, offs4)):
            nc.sync.dma_start(tile[:], src)

        nc.vector.memset(fours[:], 4.0)

        wq_plane = sb.tile([P, K], U8, align_bytes=64)
        wq_codes = sb.tile([P, K], U32, align_bytes=64)
        nc.vector.tensor_copy(
            out=wq_plane[:].rearrange("p (j m) -> p j m", j=PACK), in_=wq_plane_raw[:].rearrange("p (m j) -> p j m", j=PACK)
        )
        nc.scalar.copy(
            out=wq_codes[:].rearrange("p (j m) -> p m j", j=PACK), in_=wq_raw[:].rearrange("p (m j) -> p m j", j=PACK)
        )

        states_bf = [sb.tile([P, Q // 2, PACK], BF16, name=f"states_bf{h}", tag=f"states_bf{h}", align_bytes=64) for h in range(2)]
        states_codes = sb.tile([P, Q], U32, align_bytes=64)
        states_plane = sb.tile([P, Q], U8, align_bytes=64)
        row_halves = [slice(h * Q // 2, (h + 1) * Q // 2) for h in range(2)]
        for half_bf, rows in zip(states_bf, row_halves):
            nc.vector.tensor_copy(out=half_bf[:], in_=states_raw[:, :, rows].rearrange("p j q -> p q j"))
        for half_bf, rows in zip(states_bf, row_halves):
            nc.vector.quantize_mx(
                out=states_codes[:, rows].bitcast(FP8X4),
                scales=states_plane[:, rows],
                in_=half_bf[:].rearrange("p q j -> p (q j)"),
            )
        given = sb.tile([P, T], F32, tag="states_bf1", align_bytes=64)
        nc.vector.memset(given[:], 0.0)

        qv_ps = ps.tile([P, PACK, Q], F32)
        for j in range(PACK):
            cols = slice(j * P, (j + 1) * P)
            nc.tensor.matmul_mx(
                out=qv_ps[:, j, :],
                lhsT=wq_codes[:, cols].bitcast(FP8X4),
                lhsT_scale=wq_plane[:, cols],
                rhs=states_codes[:].bitcast(FP8X4),
                rhs_scale=states_plane[:],
                start=True,
                stop=True,
            )
        score_ps = [ps.tile([P, BANK], F32, name=f"score_ps{b}", tag=f"score_ps{b}") for b in range(T // BANK)]
        for b in range(T // BANK):
            cols = slice(b * BANK, (b + 1) * BANK)
            nc.tensor.matmul_mx(
                out=score_ps[b][:],
                lhsT=states_codes[:].bitcast(FP8X4),
                lhsT_scale=states_plane[:],
                rhs=tags_codes[:, cols].bitcast(FP8X4),
                rhs_scale=tags_plane[:, cols],
                start=True,
                stop=False,
            )

        qv_bf = sb.tile([P, Q, PACK], BF16, align_bytes=64)
        qv_codes = sb.tile([P, Q], U32, align_bytes=64)
        qv_plane = sb.tile([P, Q], U8, align_bytes=64)
        for rows in row_halves:
            nc.scalar.copy(out=qv_bf[:, rows, :], in_=qv_ps[:, :, rows].rearrange("p j q -> p q j"))
            nc.vector.quantize_mx(
                out=qv_codes[:, rows].bitcast(FP8X4),
                scales=qv_plane[:, rows],
                in_=qv_bf[:, rows, :].rearrange("p q j -> p (q j)"),
            )

        scores = sb.tile([P, T], F32)
        bank_max = sb.tile([P, T // BANK], F32, tag="bank_max")
        neg_max = sb.tile([P, 1], F32)
        for b in range(T // BANK):
            cols = slice(b * BANK, (b + 1) * BANK)
            nc.tensor.matmul_mx(
                out=score_ps[b][:],
                lhsT=qv_codes[:].bitcast(FP8X4),
                lhsT_scale=qv_plane[:],
                rhs=keys_codes[:, 2 * b * BANK : 2 * (b + 1) * BANK].bitcast(FP4X4),
                rhs_scale=keys_plane[:, cols],
                start=False,
                stop=True,
            )
            nc.vector.tensor_scalar(
                out=scores[:, cols], in0=score_ps[b][:], scalar1=1.0, scalar2=None, op0=ALU.mult, op1=ALU.max,
                accum_out=bank_max[:, b : b + 1],
            )
        nc.vector.tensor_reduce(out=neg_max[:], in_=bank_max[:], axis=AXIS.X, op=ALU.max, negate=True)
        taken = sb.tile([P, T], F32, tag="bank_max")
        nc.vector.memset(taken[:], 0.0)

        pieces = [slice(c * PIECE, (c + 1) * PIECE) for c in range(TURNED // PIECE)]
        turned_ps = [ps.tile([P, PIECE], F32, name=f"turned_ps{c}") for c in range(TURNED // PIECE)]

        def turn_into(bank, src, first):
            for c in range(PIECE // P):
                cols = slice(c * P, (c + 1) * P)
                nc.tensor.matmul(
                    bank[:, cols], lhsT=src[:, cols], rhs=identity[:], is_transpose=True,
                    start=(first and c == 0), stop=(not first and c == PIECE // P - 1),
                )

        for bank, cols in zip(turned_ps, pieces):
            turn_into(bank, scores[:, cols], True)

        halves = [(slice(h * HALF, (h + 1) * HALF), slice(h * HALF // 16, (h + 1) * HALF // 16)) for h in range(2)]
        e1 = sb.tile([P, SLOTS], F32)
        for slots, entries in halves:
            nc.scalar.activation(
                out=e1[:, slots], in_=scores[:].indirect(fetch_list[:, entries]), func=ACT.Exp, bias=neg_max[:]
            )
        for slots, entries in halves:
            nc.vector.tensor_tensor(given[:].indirect(give_list[:, entries]), e1[:, slots], fours[:], ALU.mult)
        minus_four_e1 = sb.tile([P, SLOTS], F32)
        nc.scalar.activation(minus_four_e1[:], e1[:], ACT.Copy, scale=-4.0)
        nc.vector.tensor_copy(taken[:].indirect(take_list[:]), minus_four_e1[:])
        cc = sb.tile([P, T], F32)
        turned = sb.tile([P, TURNED], F32)
        for bank, cols in zip(turned_ps, pieces):
            turn_into(bank, given[:, cols], False)
            nc.scalar.copy(out=turned[:, cols], in_=bank[:])
        rest = slice(TURNED, T)
        with_given = sb.tile([P, T - TURNED], F32)
        nc.vector.tensor_tensor(with_given[:], scores[:, rest], given[:, rest], ALU.add)
        nc.gpsimd.tensor_tensor(cc[:, rest], with_given[:], taken[:, rest], ALU.add)
        for b, first in enumerate(range(0, TURNED, BANK)):
            width = min(BANK, TURNED - first)
            with_given_ps = ps.tile([P, width], F32, name=f"with_given_ps{b}", tag=f"score_ps{b}")
            for c in range(0, width, P):
                nc.tensor.transpose(with_given_ps[:, c : c + P], turned[:, first + c : first + c + P], identity[:])
            cols = slice(first, first + width)
            nc.vector.tensor_tensor(cc[:, cols], with_given_ps[:], taken[:, cols], ALU.add)

        picked = [sb.tile([P, HALF], F32, name=f"picked{h}") for h in range(2)]
        nc.vector.tensor_copy(picked[0][:], cc[:].indirect(out_list[:, halves[0][1]]))
        nc.scalar.activation(picked[1][:], cc[:].indirect(out_list[:, halves[1][1]]), ACT.Copy)
        nc.sync.dma_start(out=out[:, halves[0][0]], in_=picked[0][:])
        nc.scalar.dma_start(out=out[:, halves[1][0]], in_=picked[1][:])
